import numpy as np
import ml_dtypes


def mxq(x, axis, fmt="e4m3"):
    dtype, down = {"e4m3": (ml_dtypes.float8_e4m3fn, 7), "e5m2": (ml_dtypes.float8_e5m2, 14)}[fmt]
    v = np.moveaxis(np.asarray(x, np.float32).astype(ml_dtypes.bfloat16).astype(np.float64), axis, -1)
    blocks = v.reshape(v.shape[:-1] + (-1, 32))
    amax = np.abs(blocks).max(-1, keepdims=True)
    byte = np.maximum(np.where(amax > 0, np.frexp(amax)[1] - 1 + 127, 0) - down, 1)
    scale = np.exp2(byte - 127.0)
    codes = (blocks / scale).astype(np.float32).astype(dtype).astype(np.float64)
    return np.moveaxis((codes * scale).reshape(v.shape), -1, axis)


WIDE = False


def mx_kscale(k):
    if not WIDE:
        return np.ones(k)
    levels = np.array([10, -10, 5, -5, 0])
    if k % 512:
        return np.exp2(np.random.permutation(np.resize(levels, k // 32))).repeat(32)
    a = np.empty((k // 512, 16))
    for p in range(k // 512):
        a[p, :8] = np.random.permutation(np.resize(levels, 8))
        for g in range(8):
            far = levels[np.abs(levels - a[p, g]) >= 10]
            a[p, g + 8] = far[np.random.randint(len(far))]
    return np.exp2(a.ravel()).repeat(32)


def f64(x):
    return np.asarray(x).astype(np.float64)


def striped(idx):
    return np.tile(np.asarray(idx).reshape(-1, 16).T, (8, 1)).astype(np.uint16)


def unstriped(offs):
    return offs[:16].T.reshape(-1).astype(np.int64)


E2M1 = np.array([0.0, 0.5, 1.0, 1.5, 2.0, 3.0, 4.0, 6.0, -0.0, -0.5, -1.0, -1.5, -2.0, -3.0, -4.0, -6.0])


def pack_weight(w, fmt):
    k, n = w.shape
    w = f64(np.asarray(w, np.float32).astype(ml_dtypes.bfloat16)).reshape(k // 32, 32, n)
    amax = np.abs(w).max(1)
    if fmt == "e4m3":
        byte = np.frexp(amax)[1] - 1 + 127 - 7
    else:
        mant, ex = np.frexp(amax / 6.0)
        byte = np.where(mant > 0.5, ex, ex - 1) + 127
    byte = np.clip(np.where(amax > 0, byte, 1), 1, 254)
    scaled = (w * np.exp2(127.0 - byte)[:, None, :]).reshape(k, n).astype(np.float32)
    by_word = np.ascontiguousarray(scaled.reshape(k // 512, 128, 4, n).transpose(0, 1, 3, 2))
    if fmt == "e4m3":
        words = by_word.astype(ml_dtypes.float8_e4m3fn).view(np.uint8)
    else:
        c = by_word.astype(ml_dtypes.float4_e2m1fn).view(np.uint8) & 0xF
        words = (c[..., 0::2] | (c[..., 1::2] << 4)).reshape(k // 512, 128, 2 * n)
    return np.ascontiguousarray(words), np.ascontiguousarray(byte.astype(np.uint8).reshape(k // 512, 16, n))


def unpack_weight(words, scales, fmt):
    g, _, n = scales.shape
    words = np.ascontiguousarray(words).reshape(g, 128, n, -1)
    if fmt == "e4m3":
        vals = words.view(ml_dtypes.float8_e4m3fn).astype(np.float64)
    else:
        nib = np.empty((g, 128, n, 4), np.uint8)
        nib[..., 0::2] = words & 0xF
        nib[..., 1::2] = words >> 4
        vals = E2M1[nib]
    vals = vals * np.repeat(np.exp2(scales.astype(np.float64) - 127.0), 8, axis=1)[..., None]
    return vals.transpose(0, 1, 3, 2).reshape(g * 512, n)


def bf(x):
    return np.asarray(x, np.float32).astype(ml_dtypes.bfloat16)


def planes(Y):
    r, m = Y.shape
    b = f64(bf(Y)).reshape(r // 32, 32, m)
    amax = np.abs(b).max(1)
    byte = np.clip(np.where(amax > 0, np.frexp(amax)[1] - 1 + 127 - 7, 1), 1, 254)
    codes = (b * np.exp2(127.0 - byte)[:, None, :]).reshape(r, m).astype(np.float32).astype(ml_dtypes.float8_e4m3fn).view(np.uint8)
    words = codes.reshape(r // 512, 128, 4, m).transpose(0, 1, 3, 2)
    return np.ascontiguousarray(words), np.ascontiguousarray(byte.astype(np.uint8).reshape(r // 512, 16, m))


K, T, J, R, N = 512, 1024, 512, 512, 512


def setup_inputs():
    n = np.random.standard_normal
    idx = np.random.permutation(T)[:J]
    fk = mx_kscale(K)
    fr = mx_kscale(R)
    xtp = pack_weight(n((K, T)) / fk[:, None], "e2m1")
    wap = pack_weight(n((K, R)) * 1 / np.sqrt(K) * fk[:, None] * fr, "e4m3")
    wbp = pack_weight(n((R, N)) * 1 / np.sqrt(R) / fr[:, None], "e2m1")
    return {
        "xt_words": xtp[0],
        "xt_scales": xtp[1],
        "wa_words": wap[0],
        "wa_scales": wap[1],
        "dc": (np.random.uniform(0.3, 0.9, (R, 1))).astype(np.float32),
        "wb_words": wbp[0],
        "wb_scales": wbp[1],
        "ga": (np.random.uniform(0.4, 1.2, (1, J))).astype(np.float32),
        "offs": striped(idx),
    }


def reference(xt_words, xt_scales, wa_words, wa_scales, dc, wb_words, wb_scales, ga, offs):
    idx = unstriped(offs)
    xtu = unpack_weight(xt_words, xt_scales, "e2m1")
    wau = unpack_weight(wa_words, wa_scales, "e4m3")
    wbu = unpack_weight(wb_words, wb_scales, "e2m1")
    xtidxg = xtu[:, idx]
    a = wau.T @ xtidxg
    h1 = np.maximum(a, 0.0)
    hp = np.pad(h1, ((0, 0), (1, 0)))[:, :J]
    hid = h1 + f64(dc) * hp
    hidq = mxq(hid, 0, "e4m3")
    p = wbu.T @ hidq
    pw = p * f64(ga)
    y = np.zeros((N, T))
    y[:, idx] = pw
    words, scales = planes(y)
    return y, words, scales

@@ -1,0 +1,218 @@
+from contextlib import ExitStack
+
+import concourse.mybir as mybir
+
+K, T, J, R, N = 512, 1024, 512, 512, 512
+FLOPS = 2 * K * R * J + 2 * R * N * J
+
+F32 = mybir.dt.float32
+BF16 = mybir.dt.bfloat16
+I32 = mybir.dt.int32
+U32 = mybir.dt.uint32
+U16 = mybir.dt.uint16
+U8 = mybir.dt.uint8
+FP8X4 = mybir.dt.float8_e4m3fn_x4
+FP4X4 = mybir.dt.float4_e2m1fn_x4
+MULT = mybir.AluOpType.mult
+ADD = mybir.AluOpType.add
+RELU = mybir.ActivationFunctionType.Relu
+COPY = mybir.ActivationFunctionType.Copy
+
+P = 128
+PACK = 4
+CHUNKS = (128, 128, 128, 128)
+BANK = 512
+
+
+def load_scale_rows(nc, plane, scales):
+    rows = scales[0].bitcast(I32).rearrange("(q r) c -> r q c", r=4)
+    for r in range(4):
+        nc.sync.dma_start(out=plane[r:P:32, :].bitcast(I32), in_=rows[r])
+
+
+def deal_columns(nc, dealt, plain):
+    nc.vector.tensor_copy(
+        out=dealt.rearrange("p (t m) -> p m t", t=PACK),
+        in_=plain.rearrange("p (m t) -> p m t", t=PACK),
+    )
+
+
+def tile_moe_expert_hidden_taps_scattered_pl_kernel(
+    tc, xt_words, xt_scales, wa_words, wa_scales, dc, wb_words, wb_scales, ga, offs, out_0, out_1, out_2
+):
+    nc = tc.nc
+    with ExitStack() as ctx:
+        sb = ctx.enter_context(tc.tile_pool(name="sb", bufs=1))
+        reuse = ctx.enter_context(tc.tile_pool(name="reuse", bufs=1))
+        ps = ctx.enter_context(tc.psum_pool(name="ps", bufs=1))
+
+        offsets = sb.tile([P, J // 16], U16, name="offsets")
+        x_w = sb.tile([P, T], U16, name="x_w", align_bytes=64)
+        x_s = sb.tile([P, T], U8, name="x_s", align_bytes=64)
+        wa_w = sb.tile([P, R], I32, name="wa_w", tag="wa_then_ga", align_bytes=64)
+        wa_s = reuse.tile([P, R], U8, name="wa_s", align_bytes=64, offset=0)
+        wb_w = sb.tile([P, N], U16, name="wb_w", align_bytes=64)
+        wb_s = sb.tile([P, N], U8, name="wb_s", align_bytes=64)
+        wa_wd = sb.tile([P, R], I32, name="wa_wd", align_bytes=64)
+        wa_sd = sb.tile([P, R], U8, name="wa_sd", align_bytes=64)
+        wb_wd = sb.tile([P, N], U16, name="wb_wd", align_bytes=64)
+        wb_sd = sb.tile([P, N], U8, name="wb_sd", align_bytes=64)
+        dc_sb = sb.tile([P, PACK], F32, name="dc_sb")
+        h1 = sb.tile([P, PACK, J + 4], F32, name="h1", align_bytes=64)
+        p_sb = sb.tile([P, PACK, J], F32, name="p_sb", align_bytes=64)
+        y = [sb.tile([P, T], F32, name="y%d" % t, align_bytes=64) for t in range(PACK)]
+        quarter = T // 4
+        pairs = [sb.tile([P, 2, quarter, 2], BF16, name="pairs%d" % q, align_bytes=64) for q in range(4)]
+        y_bf = [sb.tile([P, quarter, PACK], BF16, name="y_bf%d" % q, align_bytes=64) for q in range(4)]
+        y_w = sb.tile([P, T], U32, name="y_w", align_bytes=64)
+        y_s = sb.tile([P, T], U8, name="y_s", align_bytes=64)
+
+        for plane in (x_s, wa_s, wb_s):
+            nc.vector.memset(plane[:].bitcast(I32), 0)
+        nc.vector.memset(h1[:, :, 3:4], 0.0)
+
+        nc.sync.dma_start(offsets[:], offs)
+        nc.sync.dma_start(out=x_w[:].bitcast(I32), in_=xt_words[0].bitcast(I32))
+        load_scale_rows(nc, x_s, xt_scales)
+        nc.sync.dma_start(out=wa_w[:], in_=wa_words[0].rearrange("p n t -> p (n t)").bitcast(I32))
+        load_scale_rows(nc, wa_s, wa_scales)
+        nc.gpsimd.dma_start(out=dc_sb[:], in_=dc.rearrange("(p t) o -> p (t o)", t=PACK))
+        nc.gpsimd.dma_start(out=wb_w[:].bitcast(I32), in_=wb_words[0].bitcast(I32))
+        load_scale_rows(nc, wb_s, wb_scales)
+
+        starts = [sum(CHUNKS[:c]) for c in range(len(CHUNKS))]
+        gathered = []
+        for c, n in enumerate(CHUNKS):
+            lst = offsets[:, starts[c] // 16 : (starts[c] + n) // 16]
+            if c == 2:
+                g_w = reuse.tile([P, n], U16, name="g_w%d" % c, align_bytes=64, offset=0)
+            else:
+                g_w = sb.tile([P, n], U16, name="g_w%d" % c, align_bytes=64)
+            if c >= 2:
+                g_s = reuse.tile([P, n], U8, name="g_s%d" % c, align_bytes=64, offset=128 * c)
+            else:
+                g_s = sb.tile([P, n], U8, name="g_s%d" % c, align_bytes=64)
+            nc.vector.tensor_copy(g_w[:], x_w[:].indirect(lst))
+            nc.vector.tensor_copy(g_s[:], x_s[:].indirect(lst))
+            gathered.append((g_w, g_s))
+            if c == 0:
+                deal_columns(nc, wa_wd[:], wa_w[:])
+                deal_columns(nc, wa_sd[:], wa_s[:])
+                ga_sb = sb.tile([P, J], F32, name="ga_sb", tag="wa_then_ga", align_bytes=64)
+                nc.sync.dma_start(out=ga_sb[:], in_=ga[0].partition_broadcast(P))
+        deal_columns(nc, wb_wd[:], wb_w[:])
+        deal_columns(nc, wb_sd[:], wb_s[:])
+
+        for c, n in enumerate(CHUNKS):
+            j0, j1 = starts[c], starts[c] + n
+            g_w, g_s = gathered[c]
+            per_bank = BANK // n
+            for t0 in range(0, PACK, per_bank):
+                acc = ps.tile([P, per_bank, n], F32, name="a%d_%d" % (c, t0))
+                for u in range(per_bank):
+                    cols = slice((t0 + u) * P, (t0 + u + 1) * P)
+                    nc.tensor.matmul_mx(
+                        out=acc[:, u, :],
+                        lhsT=wa_wd[:, cols].bitcast(FP8X4),
+                        lhsT_scale=wa_sd[:, cols],
+                        rhs=g_w[:].bitcast(FP4X4),
+                        rhs_scale=g_s[:],
+                        start=True,
+                        stop=True,
+                    )
+                nc.scalar.activation(out=h1[:, t0 : t0 + per_bank, 4 + j0 : 4 + j1], in_=acc[:], func=RELU)
+            hid_rows = sb.tile([P, PACK, n], BF16, name="hid_rows%d" % c, align_bytes=64)
+            for t in range(PACK):
+                nc.vector.scalar_tensor_tensor(
+                    out=hid_rows[:, t, :],
+                    in0=h1[:, t, 3 + j0 : 3 + j1],
+                    scalar=dc_sb[:, t : t + 1],
+                    in1=h1[:, t, 4 + j0 : 4 + j1],
+                    op0=MULT,
+                    op1=ADD,
+                )
+            hid = sb.tile([P, n, PACK], BF16, name="hid%d" % c, align_bytes=64)
+            nc.scalar.copy(
+                out=hid[:].rearrange("p (c i) t -> p c t i", i=4),
+                in_=hid_rows[:].rearrange("p t (c i) -> p c t i", i=4),
+            )
+            h_w = sb.tile([P, n], U32, name="h_w%d" % c, align_bytes=64)
+            h_s = sb.tile([P, n], U8, name="h_s%d" % c, align_bytes=64)
+            nc.vector.quantize_mx(out=h_w[:].bitcast(FP8X4), scales=h_s[:], in_=hid[:].rearrange("p j t -> p (j t)"))
+            for t0 in range(0, PACK, per_bank):
+                acc = ps.tile([P, per_bank, n], F32, name="p%d_%d" % (c, t0))
+                for u in range(per_bank):
+                    cols = slice((t0 + u) * P, (t0 + u + 1) * P)
+                    nc.tensor.matmul_mx(
+                        out=acc[:, u, :],
+                        lhsT=wb_wd[:, cols].bitcast(FP4X4),
+                        lhsT_scale=wb_sd[:, cols],
+                        rhs=h_w[:].bitcast(FP8X4),
+                        rhs_scale=h_s[:],
+                        start=True,
+                        stop=True,
+                    )
+                nc.scalar.copy(out=p_sb[:, t0 : t0 + per_bank, j0:j1], in_=acc[:])
+
+        for t in range(PACK):
+            nc.vector.memset(y[t][:].bitcast(I32), 0)
+
+        out_rows = out_0.rearrange("(p t) c -> p t c", t=PACK)
+
+        def scatter(t, j0, n):
+            nc.vector.tensor_tensor(
+                y[t][:].indirect(offsets[:, j0 // 16 : (j0 + n) // 16]),
+                p_sb[:, t, j0 : j0 + n],
+                ga_sb[:, j0 : j0 + n],
+                MULT,
+            )
+
+        def cast(t, q, engine_copy):
+            engine_copy(out=pairs[q][:, t // 2, :, t % 2], in_=y[t][:, q * quarter : (q + 1) * quarter])
+
+        for j0, n in zip(starts, CHUNKS):
+            scatter(0, j0, n)
+            scatter(1, j0, n)
+        for t in (0, 1):
+            nc.sync.dma_start(out=out_rows[:, t, :], in_=y[t][:])
+            for q in range(4):
+                cast(t, q, nc.scalar.copy)
+        scatter(2, 0, J)
+        nc.sync.dma_start(out=out_rows[:, 2, :], in_=y[2][:])
+        for q in range(4):
+            if q < 2:
+                nc.scalar.copy(
+                    out=pairs[q][:, 1, :, :],
+                    in_=y[2][:, q * quarter : (q + 1) * quarter].unsqueeze(2).to_broadcast([P, quarter, 2]),
+                )
+            else:
+                cast(2, q, nc.scalar.copy)
+        scatter(3, 0, J)
+        nc.sync.dma_start(out=out_rows[:, 3, :], in_=y[3][:])
+
+        def weave(q, engine_copy):
+            engine_copy(
+                out=y_bf[q][:].rearrange("p c t -> p (c t)").bitcast(F32).rearrange("p (c u) -> p c u", u=2),
+                in_=pairs[q][:].rearrange("p u c e -> p u (c e)").bitcast(F32).rearrange("p u c -> p c u"),
+            )
+
+        for q in (0, 1):
+            cast(3, q, nc.vector.tensor_copy)
+        for q in (0, 1):
+            weave(q, nc.vector.tensor_copy)
+        for q in (2, 3):
+            cast(3, q, nc.scalar.copy)
+            weave(q, nc.scalar.copy)
+        words_out = out_1[0].rearrange("p c t -> p (c t)").bitcast(I32)
+        for q in range(4):
+            cols = slice(q * quarter, (q + 1) * quarter)
+            nc.vector.quantize_mx(
+                out=y_w[:, cols].bitcast(FP8X4), scales=y_s[:, cols], in_=y_bf[q][:].rearrange("p c t -> p (c t)")
+            )
+            if q > 0:
+                done = slice(0 if q == 1 else q * quarter, (q + 1) * quarter)
+                nc.sync.dma_start(out=words_out[:, done], in_=y_w[:, done].bitcast(I32))
+        rows_out = out_2[0].bitcast(I32).rearrange("(q r) c -> r q c", r=4)
+        for r in range(4):
+            queue = nc.scalar if r % 2 else nc.sync
+            queue.dma_start(out=rows_out[r], in_=y_s[r:P:32, :].bitcast(I32))

@@ -20,8 +20,9 @@ COPY = mybir.ActivationFunctionType.Copy
 
 P = 128
 PACK = 4
-CHUNKS = (128, 128, 128, 128)
-BANK = 512
+CHUNK = 128
+GATHERS = (128, 128, 256)
+QUARTER = T // 4
 
 
 def load_scale_rows(nc, plane, scales):
@@ -43,119 +44,140 @@ def tile_moe_expert_hidden_taps_scattered_pl_kernel(
     nc = tc.nc
     with ExitStack() as ctx:
         sb = ctx.enter_context(tc.tile_pool(name="sb", bufs=1))
-        reuse = ctx.enter_context(tc.tile_pool(name="reuse", bufs=1))
+        late = ctx.enter_context(tc.tile_pool(name="late", bufs=1))
         ps = ctx.enter_context(tc.psum_pool(name="ps", bufs=1))
 
         offsets = sb.tile([P, J // 16], U16, name="offsets")
         x_w = sb.tile([P, T], U16, name="x_w", align_bytes=64)
         x_s = sb.tile([P, T], U8, name="x_s", align_bytes=64)
-        wa_w = sb.tile([P, R], I32, name="wa_w", tag="wa_then_ga", align_bytes=64)
-        wa_s = reuse.tile([P, R], U8, name="wa_s", align_bytes=64, offset=0)
-        wb_w = sb.tile([P, N], U16, name="wb_w", align_bytes=64)
-        wb_s = sb.tile([P, N], U8, name="wb_s", align_bytes=64)
-        wa_wd = sb.tile([P, R], I32, name="wa_wd", align_bytes=64)
-        wa_sd = sb.tile([P, R], U8, name="wa_sd", align_bytes=64)
+        wa_w = sb.tile([P, R], I32, name="wa_w", align_bytes=64)
+        w_s = sb.tile([P, R + N], U8, name="w_s", align_bytes=64)
+        wa_s, wb_s = w_s[:, :R], w_s[:, R:]
+        zeros = late.tile([P, P], F32, name="zeros", align_bytes=64, offset=768)
+        wb_w = late.tile([P, N], U16, name="wb_w", align_bytes=64, offset=0)
+        dc_sb = late.tile([P, PACK], F32, name="dc_sb", align_bytes=64, offset=1024)
+        ga_sb = late.tile([P, J], F32, name="ga_sb", align_bytes=64, offset=1088)
         wb_wd = sb.tile([P, N], U16, name="wb_wd", align_bytes=64)
         wb_sd = sb.tile([P, N], U8, name="wb_sd", align_bytes=64)
-        dc_sb = sb.tile([P, PACK], F32, name="dc_sb")
-        h1 = sb.tile([P, PACK, J + 4], F32, name="h1", align_bytes=64)
+        ident = sb.tile([P, P], F32, name="ident", align_bytes=64)
+        tap = sb.tile([P, PACK, J], F32, name="tap", align_bytes=64)
         p_sb = sb.tile([P, PACK, J], F32, name="p_sb", align_bytes=64)
-        y = [sb.tile([P, T], F32, name="y%d" % t, align_bytes=64) for t in range(PACK)]
-        quarter = T // 4
-        pairs = [sb.tile([P, 2, quarter, 2], BF16, name="pairs%d" % q, align_bytes=64) for q in range(4)]
-        y_bf = [sb.tile([P, quarter, PACK], BF16, name="y_bf%d" % q, align_bytes=64) for q in range(4)]
+        pairs = [sb.tile([P, 2, QUARTER, 2], BF16, name="pairs%d" % q, align_bytes=64) for q in range(4)]
+        y_bf = [sb.tile([P, QUARTER, PACK], BF16, name="y_bf%d" % q, align_bytes=64) for q in range(4)]
         y_w = sb.tile([P, T], U32, name="y_w", align_bytes=64)
         y_s = sb.tile([P, T], U8, name="y_s", align_bytes=64)
 
-        for plane in (x_s, wa_s, wb_s):
-            nc.vector.memset(plane[:].bitcast(I32), 0)
-        nc.vector.memset(h1[:, :, 3:4], 0.0)
+        nc.vector.memset(x_s[:].bitcast(I32), 0)
+        nc.vector.memset(w_s[:].bitcast(I32), 0)
+        nc.gpsimd.memset(zeros[:], 0.0)
+        nc.gpsimd.affine_select(
+            out=ident[:],
+            in_=zeros[:],
+            compare_op=mybir.AluOpType.not_equal,
+            fill=1.0,
+            base=0,
+            pattern=[[-1, P]],
+            channel_multiplier=1,
+        )
+        nc.gpsimd.memset(tap[:, :, 0:1], 0.0)
 
         nc.sync.dma_start(offsets[:], offs)
         nc.sync.dma_start(out=x_w[:].bitcast(I32), in_=xt_words[0].bitcast(I32))
-        load_scale_rows(nc, x_s, xt_scales)
         nc.sync.dma_start(out=wa_w[:], in_=wa_words[0].rearrange("p n t -> p (n t)").bitcast(I32))
+        load_scale_rows(nc, x_s, xt_scales)
         load_scale_rows(nc, wa_s, wa_scales)
-        nc.gpsimd.dma_start(out=dc_sb[:], in_=dc.rearrange("(p t) o -> p (t o)", t=PACK))
-        nc.gpsimd.dma_start(out=wb_w[:].bitcast(I32), in_=wb_words[0].bitcast(I32))
+        nc.sync.dma_start(out=dc_sb[:], in_=dc.rearrange("(p t) o -> p (t o)", t=PACK))
+        nc.sync.dma_start(out=wb_w[:].bitcast(I32), in_=wb_words[0].bitcast(I32))
         load_scale_rows(nc, wb_s, wb_scales)
+        nc.sync.dma_start(out=ga_sb[:], in_=ga[0].partition_broadcast(P))
 
-        starts = [sum(CHUNKS[:c]) for c in range(len(CHUNKS))]
-        gathered = []
-        for c, n in enumerate(CHUNKS):
-            lst = offsets[:, starts[c] // 16 : (starts[c] + n) // 16]
-            if c == 2:
-                g_w = reuse.tile([P, n], U16, name="g_w%d" % c, align_bytes=64, offset=0)
-            else:
-                g_w = sb.tile([P, n], U16, name="g_w%d" % c, align_bytes=64)
-            if c >= 2:
-                g_s = reuse.tile([P, n], U8, name="g_s%d" % c, align_bytes=64, offset=128 * c)
-            else:
-                g_s = sb.tile([P, n], U8, name="g_s%d" % c, align_bytes=64)
+        tokens = []
+        j0 = 0
+        for g, n in enumerate(GATHERS):
+            lst = offsets[:, j0 // 16 : (j0 + n) // 16]
+            g_w = sb.tile([P, n], U16, name="g_w%d" % g, align_bytes=64)
+            g_s = sb.tile([P, n], U8, name="g_s%d" % g, align_bytes=64)
             nc.vector.tensor_copy(g_w[:], x_w[:].indirect(lst))
             nc.vector.tensor_copy(g_s[:], x_s[:].indirect(lst))
-            gathered.append((g_w, g_s))
-            if c == 0:
-                deal_columns(nc, wa_wd[:], wa_w[:])
-                deal_columns(nc, wa_sd[:], wa_s[:])
-                ga_sb = sb.tile([P, J], F32, name="ga_sb", tag="wa_then_ga", align_bytes=64)
-                nc.sync.dma_start(out=ga_sb[:], in_=ga[0].partition_broadcast(P))
-        deal_columns(nc, wb_wd[:], wb_w[:])
-        deal_columns(nc, wb_sd[:], wb_s[:])
+            for c0 in range(0, n, CHUNK):
+                tokens.append((g_w[:, c0 : c0 + CHUNK], g_s[:, c0 : c0 + CHUNK]))
+            j0 = j0 + n
 
-        for c, n in enumerate(CHUNKS):
-            j0, j1 = starts[c], starts[c] + n
-            g_w, g_s = gathered[c]
-            per_bank = BANK // n
-            for t0 in range(0, PACK, per_bank):
-                acc = ps.tile([P, per_bank, n], F32, name="a%d_%d" % (c, t0))
-                for u in range(per_bank):
-                    cols = slice((t0 + u) * P, (t0 + u + 1) * P)
-                    nc.tensor.matmul_mx(
-                        out=acc[:, u, :],
-                        lhsT=wa_wd[:, cols].bitcast(FP8X4),
-                        lhsT_scale=wa_sd[:, cols],
-                        rhs=g_w[:].bitcast(FP4X4),
-                        rhs_scale=g_s[:],
-                        start=True,
-                        stop=True,
-                    )
-                nc.scalar.activation(out=h1[:, t0 : t0 + per_bank, 4 + j0 : 4 + j1], in_=acc[:], func=RELU)
-            hid_rows = sb.tile([P, PACK, n], BF16, name="hid_rows%d" % c, align_bytes=64)
-            for t in range(PACK):
-                nc.vector.scalar_tensor_tensor(
-                    out=hid_rows[:, t, :],
-                    in0=h1[:, t, 3 + j0 : 3 + j1],
-                    scalar=dc_sb[:, t : t + 1],
-                    in1=h1[:, t, 4 + j0 : 4 + j1],
-                    op0=MULT,
-                    op1=ADD,
-                )
-            hid = sb.tile([P, n, PACK], BF16, name="hid%d" % c, align_bytes=64)
-            nc.scalar.copy(
-                out=hid[:].rearrange("p (c i) t -> p c t i", i=4),
-                in_=hid_rows[:].rearrange("p t (c i) -> p c t i", i=4),
+        chunks = J // CHUNK
+        hidden = {}
+
+        def first_layer(c):
+            j0, j1 = c * CHUNK, (c + 1) * CHUNK
+            g_w, g_s = tokens[c]
+            a_t = ps.tile([P, R], F32, name="a_t", bufs=2)
+            nc.tensor.matmul_mx(
+                out=a_t[:],
+                lhsT=g_w.bitcast(FP4X4),
+                lhsT_scale=g_s,
+                rhs=wa_w[:].bitcast(FP8X4),
+                rhs_scale=wa_s,
+                start=True,
+                stop=True,
             )
-            h_w = sb.tile([P, n], U32, name="h_w%d" % c, align_bytes=64)
-            h_s = sb.tile([P, n], U8, name="h_s%d" % c, align_bytes=64)
-            nc.vector.quantize_mx(out=h_w[:].bitcast(FP8X4), scales=h_s[:], in_=hid[:].rearrange("p j t -> p (j t)"))
-            for t0 in range(0, PACK, per_bank):
-                acc = ps.tile([P, per_bank, n], F32, name="p%d_%d" % (c, t0))
-                for u in range(per_bank):
-                    cols = slice((t0 + u) * P, (t0 + u + 1) * P)
-                    nc.tensor.matmul_mx(
-                        out=acc[:, u, :],
-                        lhsT=wb_wd[:, cols].bitcast(FP4X4),
-                        lhsT_scale=wb_sd[:, cols],
-                        rhs=h_w[:].bitcast(FP8X4),
-                        rhs_scale=h_s[:],
-                        start=True,
-                        stop=True,
+            h_t = sb.tile([P, PACK, P], F32, name="h_t", bufs=2, align_bytes=64)
+            nc.scalar.activation(out=h_t[:], in_=a_t[:].rearrange("j (m t) -> j t m", t=PACK), func=RELU)
+            h1 = ps.tile([P, PACK, CHUNK], F32, name="h1", bufs=3)
+            for t in range(PACK):
+                nc.tensor.transpose(h1[:, t, :], h_t[:, t, :], ident[:])
+            kept = min(j1, J - 1) - j0
+            for t in range(PACK):
+                shifted = tap[:, t, j0 + 1 : j0 + 1 + kept]
+                if c == 0:
+                    nc.vector.tensor_scalar(
+                        out=shifted, in0=h1[:, t, :kept], scalar1=dc_sb[:, t : t + 1], scalar2=None, op0=MULT
                     )
-                nc.scalar.copy(out=p_sb[:, t0 : t0 + per_bank, j0:j1], in_=acc[:])
+                else:
+                    nc.scalar.activation(out=shifted, in_=h1[:, t, :kept], func=COPY, scale=dc_sb[:, t : t + 1])
+            hid = sb.tile([P, CHUNK, PACK], BF16, name="hid", align_bytes=64, tag="hid%d" % c)
+            nc.vector.tensor_tensor(
+                out=hid[:].rearrange("p (c i) t -> p c t i", i=4),
+                in0=h1[:].rearrange("p t (c i) -> p c t i", i=4),
+                in1=tap[:, :, j0:j1].rearrange("p t (c i) -> p c t i", i=4),
+                op=ADD,
+            )
+            h_w = sb.tile([P, CHUNK], U32, name="h_w", align_bytes=64, tag="h_w%d" % c)
+            h_s = sb.tile([P, CHUNK], U8, name="h_s%d" % c, align_bytes=64)
+            nc.vector.quantize_mx(out=h_w[:].bitcast(FP8X4), scales=h_s[:], in_=hid[:].rearrange("p j t -> p (j t)"))
+            hidden[c] = (h_w, h_s)
 
+        def second_layer(c):
+            j0, j1 = c * CHUNK, (c + 1) * CHUNK
+            h_w, h_s = hidden[c]
+            acc = ps.tile([P, PACK, CHUNK], F32, name="acc", bufs=3)
+            for t in range(PACK):
+                cols = slice(t * P, (t + 1) * P)
+                nc.tensor.matmul_mx(
+                    out=acc[:, t, :],
+                    lhsT=wb_wd[:, cols].bitcast(FP4X4),
+                    lhsT_scale=wb_sd[:, cols],
+                    rhs=h_w[:].bitcast(FP8X4),
+                    rhs_scale=h_s[:],
+                    start=True,
+                    stop=True,
+                )
+            nc.scalar.copy(out=p_sb[:, :, j0:j1], in_=acc[:])
+
+        first_layer(0)
+        deal_columns(nc, wb_wd[:], wb_w[:])
+        deal_columns(nc, wb_sd[:], wb_s)
+        ahead = 2
+        for c in range(1, chunks + ahead):
+            if c < chunks:
+                first_layer(c)
+            if c >= ahead:
+                second_layer(c - ahead)
+
+        y = []
         for t in range(PACK):
-            nc.vector.memset(y[t][:].bitcast(I32), 0)
+            tag = ("y0", "y1", "hid%d" % (chunks - 1), "h_w%d" % (chunks - 1))[t]
+            y.append(sb.tile([P, T], F32, name="y%d" % t, align_bytes=64, tag=tag))
+            engine = nc.vector if t < 2 else nc.gpsimd
+            engine.memset(y[t][:].bitcast(I32), 0)
 
         out_rows = out_0.rearrange("(p t) c -> p t c", t=PACK)
 
@@ -168,11 +190,11 @@ def tile_moe_expert_hidden_taps_scattered_pl_kernel(
             )
 
         def cast(t, q, engine_copy):
-            engine_copy(out=pairs[q][:, t // 2, :, t % 2], in_=y[t][:, q * quarter : (q + 1) * quarter])
+            engine_copy(out=pairs[q][:, t // 2, :, t % 2], in_=y[t][:, q * QUARTER : (q + 1) * QUARTER])
 
-        for j0, n in zip(starts, CHUNKS):
-            scatter(0, j0, n)
-            scatter(1, j0, n)
+        for c in range(chunks):
+            scatter(0, c * CHUNK, CHUNK)
+            scatter(1, c * CHUNK, CHUNK)
         for t in (0, 1):
             nc.sync.dma_start(out=out_rows[:, t, :], in_=y[t][:])
             for q in range(4):
@@ -183,7 +205,7 @@ def tile_moe_expert_hidden_taps_scattered_pl_kernel(
             if q < 2:
                 nc.scalar.copy(
                     out=pairs[q][:, 1, :, :],
-                    in_=y[2][:, q * quarter : (q + 1) * quarter].unsqueeze(2).to_broadcast([P, quarter, 2]),
+                    in_=y[2][:, q * QUARTER : (q + 1) * QUARTER].unsqueeze(2).to_broadcast([P, QUARTER, 2]),
                 )
             else:
                 cast(2, q, nc.scalar.copy)
@@ -202,15 +224,16 @@ def tile_moe_expert_hidden_taps_scattered_pl_kernel(
             weave(q, nc.vector.tensor_copy)
         for q in (2, 3):
             cast(3, q, nc.scalar.copy)
+        for q in (2, 3):
             weave(q, nc.scalar.copy)
         words_out = out_1[0].rearrange("p c t -> p (c t)").bitcast(I32)
         for q in range(4):
-            cols = slice(q * quarter, (q + 1) * quarter)
+            cols = slice(q * QUARTER, (q + 1) * QUARTER)
             nc.vector.quantize_mx(
                 out=y_w[:, cols].bitcast(FP8X4), scales=y_s[:, cols], in_=y_bf[q][:].rearrange("p c t -> p (c t)")
             )
             if q > 0:
-                done = slice(0 if q == 1 else q * quarter, (q + 1) * quarter)
+                done = slice(0 if q == 1 else q * QUARTER, (q + 1) * QUARTER)
                 nc.sync.dma_start(out=words_out[:, done], in_=y_w[:, done].bitcast(I32))
         rows_out = out_2[0].bitcast(I32).rearrange("(q r) c -> r q c", r=4)
         for r in range(4):

@@ -45,18 +45,20 @@ def tile_moe_expert_hidden_taps_scattered_pl_kernel(
     with ExitStack() as ctx:
         sb = ctx.enter_context(tc.tile_pool(name="sb", bufs=1))
         late = ctx.enter_context(tc.tile_pool(name="late", bufs=1))
+        shared = ctx.enter_context(tc.tile_pool(name="shared", bufs=1))
         ps = ctx.enter_context(tc.psum_pool(name="ps", bufs=1))
 
         offsets = sb.tile([P, J // 16], U16, name="offsets")
         x_w = sb.tile([P, T], U16, name="x_w", align_bytes=64)
-        x_s = sb.tile([P, T], U8, name="x_s", align_bytes=64)
+        x_s = shared.tile([P, T], U8, name="x_s", align_bytes=64, offset=4 * T - T // 2)
         wa_w = sb.tile([P, R], I32, name="wa_w", align_bytes=64)
         w_s = sb.tile([P, R + N], U8, name="w_s", align_bytes=64)
         wa_s, wb_s = w_s[:, :R], w_s[:, R:]
         zeros = late.tile([P, P], F32, name="zeros", align_bytes=64, offset=768)
         wb_w = late.tile([P, N], U16, name="wb_w", align_bytes=64, offset=0)
         dc_sb = late.tile([P, PACK], F32, name="dc_sb", align_bytes=64, offset=1024)
-        ga_sb = late.tile([P, J], F32, name="ga_sb", align_bytes=64, offset=1088)
+        ga_col = late.tile([P, PACK], F32, name="ga_col", align_bytes=64, offset=1088)
+        ga_sb = sb.tile([P, J], F32, name="ga_sb", align_bytes=64)
         wb_wd = sb.tile([P, N], U16, name="wb_wd", align_bytes=64)
         wb_sd = sb.tile([P, N], U8, name="wb_sd", align_bytes=64)
         ident = sb.tile([P, P], F32, name="ident", align_bytes=64)
@@ -87,9 +89,9 @@ def tile_moe_expert_hidden_taps_scattered_pl_kernel(
         load_scale_rows(nc, x_s, xt_scales)
         load_scale_rows(nc, wa_s, wa_scales)
         nc.sync.dma_start(out=dc_sb[:], in_=dc.rearrange("(p t) o -> p (t o)", t=PACK))
+        nc.sync.dma_start(out=ga_col[:], in_=ga.rearrange("o (p u) -> p (o u)", u=PACK))
         nc.sync.dma_start(out=wb_w[:].bitcast(I32), in_=wb_words[0].bitcast(I32))
         load_scale_rows(nc, wb_s, wb_scales)
-        nc.sync.dma_start(out=ga_sb[:], in_=ga[0].partition_broadcast(P))
 
         tokens = []
         j0 = 0
@@ -165,6 +167,10 @@ def tile_moe_expert_hidden_taps_scattered_pl_kernel(
         first_layer(0)
         deal_columns(nc, wb_wd[:], wb_w[:])
         deal_columns(nc, wb_sd[:], wb_s)
+        spread = ps.tile([P, PACK, P], F32, name="acc", bufs=3)
+        for u in range(PACK):
+            nc.tensor.transpose(spread[:, u, :], ga_col[:, u : u + 1].to_broadcast([P, P]), ident[:])
+        nc.scalar.copy(out=ga_sb[:].rearrange("p (n u) -> p n u", u=PACK), in_=spread[:].rearrange("p u n -> p n u"))
         ahead = 2
         for c in range(1, chunks + ahead):
             if c < chunks:
@@ -174,10 +180,11 @@ def tile_moe_expert_hidden_taps_scattered_pl_kernel(
 
         y = []
         for t in range(PACK):
-            tag = ("y0", "y1", "hid%d" % (chunks - 1), "h_w%d" % (chunks - 1))[t]
-            y.append(sb.tile([P, T], F32, name="y%d" % t, align_bytes=64, tag=tag))
-            engine = nc.vector if t < 2 else nc.gpsimd
-            engine.memset(y[t][:].bitcast(I32), 0)
+            if t < 2:
+                y.append(sb.tile([P, T], F32, name="y%d" % t, align_bytes=64))
+            else:
+                y.append(shared.tile([P, T], F32, name="y%d" % t, align_bytes=64, offset=4 * T * (t - 2)))
+            nc.vector.memset(y[t][:].bitcast(I32), 0)
 
         out_rows = out_0.rearrange("(p t) c -> p t c", t=PACK)
 

@@ -21,8 +21,14 @@ COPY = mybir.ActivationFunctionType.Copy
 P = 128
 PACK = 4
 CHUNK = 128
+CHUNKS = J // CHUNK
 GATHERS = (128, 128, 256)
+LIST_ROWS = 16
+AHEAD = 2
 QUARTER = T // 4
+LINE = 4
+
+WB_AT, ZEROS_AT, DC_AT, GA_AT = 0, 768, 1024, 1088
 
 
 def load_scale_rows(nc, plane, scales):
@@ -33,8 +39,8 @@ def load_scale_rows(nc, plane, scales):
 
 def deal_columns(nc, dealt, plain):
     nc.vector.tensor_copy(
-        out=dealt.rearrange("p (t m) -> p m t", t=PACK),
-        in_=plain.rearrange("p (m t) -> p m t", t=PACK),
+        out=dealt.rearrange("p (t m) -> p t m", t=PACK),
+        in_=plain.rearrange("p (m t) -> p t m", t=PACK),
     )
 
 
@@ -45,19 +51,18 @@ def tile_moe_expert_hidden_taps_scattered_pl_kernel(
     with ExitStack() as ctx:
         sb = ctx.enter_context(tc.tile_pool(name="sb", bufs=1))
         late = ctx.enter_context(tc.tile_pool(name="late", bufs=1))
-        shared = ctx.enter_context(tc.tile_pool(name="shared", bufs=1))
         ps = ctx.enter_context(tc.psum_pool(name="ps", bufs=1))
 
-        offsets = sb.tile([P, J // 16], U16, name="offsets")
+        offsets = sb.tile([P, J // LIST_ROWS], U16, name="offsets")
         x_w = sb.tile([P, T], U16, name="x_w", align_bytes=64)
-        x_s = shared.tile([P, T], U8, name="x_s", align_bytes=64, offset=4 * T - T // 2)
+        x_s = sb.tile([P, T], U8, name="x_s", align_bytes=64)
         wa_w = sb.tile([P, R], I32, name="wa_w", align_bytes=64)
         w_s = sb.tile([P, R + N], U8, name="w_s", align_bytes=64)
         wa_s, wb_s = w_s[:, :R], w_s[:, R:]
-        zeros = late.tile([P, P], F32, name="zeros", align_bytes=64, offset=768)
-        wb_w = late.tile([P, N], U16, name="wb_w", align_bytes=64, offset=0)
-        dc_sb = late.tile([P, PACK], F32, name="dc_sb", align_bytes=64, offset=1024)
-        ga_col = late.tile([P, PACK], F32, name="ga_col", align_bytes=64, offset=1088)
+        zeros = late.tile([P, P], F32, name="zeros", align_bytes=64, offset=ZEROS_AT)
+        wb_w = late.tile([P, N], U16, name="wb_w", align_bytes=64, offset=WB_AT)
+        dc_sb = late.tile([P, PACK], F32, name="dc_sb", align_bytes=64, offset=DC_AT)
+        ga_col = late.tile([P, PACK], F32, name="ga_col", align_bytes=64, offset=GA_AT)
         ga_sb = sb.tile([P, J], F32, name="ga_sb", align_bytes=64)
         wb_wd = sb.tile([P, N], U16, name="wb_wd", align_bytes=64)
         wb_sd = sb.tile([P, N], U8, name="wb_sd", align_bytes=64)
@@ -81,7 +86,7 @@ def tile_moe_expert_hidden_taps_scattered_pl_kernel(
             pattern=[[-1, P]],
             channel_multiplier=1,
         )
-        nc.gpsimd.memset(tap[:, :, 0:1], 0.0)
+        nc.vector.memset(tap[:, :, 0:1], 0.0)
 
         nc.sync.dma_start(offsets[:], offs)
         nc.sync.dma_start(out=x_w[:].bitcast(I32), in_=xt_words[0].bitcast(I32))
@@ -93,29 +98,30 @@ def tile_moe_expert_hidden_taps_scattered_pl_kernel(
         nc.sync.dma_start(out=wb_w[:].bitcast(I32), in_=wb_words[0].bitcast(I32))
         load_scale_rows(nc, wb_s, wb_scales)
 
-        tokens = []
-        j0 = 0
-        for g, n in enumerate(GATHERS):
-            lst = offsets[:, j0 // 16 : (j0 + n) // 16]
-            g_w = sb.tile([P, n], U16, name="g_w%d" % g, align_bytes=64)
-            g_s = sb.tile([P, n], U8, name="g_s%d" % g, align_bytes=64)
-            nc.vector.tensor_copy(g_w[:], x_w[:].indirect(lst))
-            nc.vector.tensor_copy(g_s[:], x_s[:].indirect(lst))
-            for c0 in range(0, n, CHUNK):
-                tokens.append((g_w[:, c0 : c0 + CHUNK], g_s[:, c0 : c0 + CHUNK]))
-            j0 = j0 + n
+        def listed(j0, count):
+            return offsets[:, j0 // LIST_ROWS : (j0 + count) // LIST_ROWS]
 
-        chunks = J // CHUNK
-        hidden = {}
+        tokens = []
+        for g, count in enumerate(GATHERS):
+            entries = listed(sum(GATHERS[:g]), count)
+            g_w = sb.tile([P, count], U16, name="g_w%d" % g, align_bytes=64)
+            g_s = sb.tile([P, count], U8, name="g_s%d" % g, align_bytes=64)
+            nc.vector.tensor_copy(g_w[:], x_w[:].indirect(entries))
+            nc.vector.tensor_copy(g_s[:], x_s[:].indirect(entries))
+            for c0 in range(0, count, CHUNK):
+                tokens.append((g_w[:, c0 : c0 + CHUNK], g_s[:, c0 : c0 + CHUNK]))
+
+        h_w = sb.tile([P, J], U32, name="h_w", align_bytes=64)
+        h_s = sb.tile([P, J], U8, name="h_s", align_bytes=64)
 
         def first_layer(c):
             j0, j1 = c * CHUNK, (c + 1) * CHUNK
-            g_w, g_s = tokens[c]
+            chunk_w, chunk_s = tokens[c]
             a_t = ps.tile([P, R], F32, name="a_t", bufs=2)
             nc.tensor.matmul_mx(
                 out=a_t[:],
-                lhsT=g_w.bitcast(FP4X4),
-                lhsT_scale=g_s,
+                lhsT=chunk_w.bitcast(FP4X4),
+                lhsT_scale=chunk_s,
                 rhs=wa_w[:].bitcast(FP8X4),
                 rhs_scale=wa_s,
                 start=True,
@@ -135,89 +141,69 @@ def tile_moe_expert_hidden_taps_scattered_pl_kernel(
                     )
                 else:
                     nc.scalar.activation(out=shifted, in_=h1[:, t, :kept], func=COPY, scale=dc_sb[:, t : t + 1])
-            hid = sb.tile([P, CHUNK, PACK], BF16, name="hid", align_bytes=64, tag="hid%d" % c)
+            hid = sb.tile([P, CHUNK, PACK], BF16, name="hid%d" % c, align_bytes=64)
             nc.vector.tensor_tensor(
-                out=hid[:].rearrange("p (c i) t -> p c t i", i=4),
-                in0=h1[:].rearrange("p t (c i) -> p c t i", i=4),
-                in1=tap[:, :, j0:j1].rearrange("p t (c i) -> p c t i", i=4),
+                out=hid[:].rearrange("p (g i) t -> p g t i", i=LINE),
+                in0=h1[:].rearrange("p t (g i) -> p g t i", i=LINE),
+                in1=tap[:, :, j0:j1].rearrange("p t (g i) -> p g t i", i=LINE),
                 op=ADD,
             )
-            h_w = sb.tile([P, CHUNK], U32, name="h_w", align_bytes=64, tag="h_w%d" % c)
-            h_s = sb.tile([P, CHUNK], U8, name="h_s%d" % c, align_bytes=64)
-            nc.vector.quantize_mx(out=h_w[:].bitcast(FP8X4), scales=h_s[:], in_=hid[:].rearrange("p j t -> p (j t)"))
-            hidden[c] = (h_w, h_s)
+            nc.vector.quantize_mx(
+                out=h_w[:, j0:j1].bitcast(FP8X4), scales=h_s[:, j0:j1], in_=hid[:].rearrange("p j t -> p (j t)")
+            )
 
-        def second_layer(c):
-            j0, j1 = c * CHUNK, (c + 1) * CHUNK
-            h_w, h_s = hidden[c]
-            acc = ps.tile([P, PACK, CHUNK], F32, name="acc", bufs=3)
-            for t in range(PACK):
+        def second_layer(row_sets, j0, j1):
+            acc = ps.tile([P, len(row_sets), j1 - j0], F32, name="acc", bufs=3)
+            for u, t in enumerate(row_sets):
                 cols = slice(t * P, (t + 1) * P)
                 nc.tensor.matmul_mx(
-                    out=acc[:, t, :],
+                    out=acc[:, u, :],
                     lhsT=wb_wd[:, cols].bitcast(FP4X4),
                     lhsT_scale=wb_sd[:, cols],
-                    rhs=h_w[:].bitcast(FP8X4),
-                    rhs_scale=h_s[:],
+                    rhs=h_w[:, j0:j1].bitcast(FP8X4),
+                    rhs_scale=h_s[:, j0:j1],
                     start=True,
                     stop=True,
                 )
-            nc.scalar.copy(out=p_sb[:, :, j0:j1], in_=acc[:])
+            nc.scalar.copy(out=p_sb[:, row_sets[0] : row_sets[-1] + 1, j0:j1], in_=acc[:])
 
         first_layer(0)
         deal_columns(nc, wb_wd[:], wb_w[:])
         deal_columns(nc, wb_sd[:], wb_s)
+
         spread = ps.tile([P, PACK, P], F32, name="acc", bufs=3)
         for u in range(PACK):
             nc.tensor.transpose(spread[:, u, :], ga_col[:, u : u + 1].to_broadcast([P, P]), ident[:])
         nc.scalar.copy(out=ga_sb[:].rearrange("p (n u) -> p n u", u=PACK), in_=spread[:].rearrange("p u n -> p n u"))
-        ahead = 2
-        for c in range(1, chunks + ahead):
-            if c < chunks:
+
+        for c in range(1, CHUNKS + AHEAD):
+            if c < CHUNKS:
                 first_layer(c)
-            if c >= ahead:
-                second_layer(c - ahead)
+            if c >= AHEAD:
+                second_layer((0, 1), (c - AHEAD) * CHUNK, (c - AHEAD + 1) * CHUNK)
+        second_layer((2,), 0, J)
+        second_layer((3,), 0, J)
 
         y = []
         for t in range(PACK):
-            if t < 2:
-                y.append(sb.tile([P, T], F32, name="y%d" % t, align_bytes=64))
-            else:
-                y.append(shared.tile([P, T], F32, name="y%d" % t, align_bytes=64, offset=4 * T * (t - 2)))
-            nc.vector.memset(y[t][:].bitcast(I32), 0)
+            y.append(sb.tile([P, T], F32, name="y%d" % t, align_bytes=64))
+            nc.gpsimd.memset(y[t][:].bitcast(I32), 0)
 
         out_rows = out_0.rearrange("(p t) c -> p t c", t=PACK)
 
-        def scatter(t, j0, n):
+        def scatter(t, j0, count):
             nc.vector.tensor_tensor(
-                y[t][:].indirect(offsets[:, j0 // 16 : (j0 + n) // 16]),
-                p_sb[:, t, j0 : j0 + n],
-                ga_sb[:, j0 : j0 + n],
+                y[t][:].indirect(listed(j0, count)),
+                p_sb[:, t, j0 : j0 + count],
+                ga_sb[:, j0 : j0 + count],
                 MULT,
             )
 
-        def cast(t, q, engine_copy):
-            engine_copy(out=pairs[q][:, t // 2, :, t % 2], in_=y[t][:, q * QUARTER : (q + 1) * QUARTER])
+        def quarter_cols(q):
+            return slice(q * QUARTER, (q + 1) * QUARTER)
 
-        for c in range(chunks):
-            scatter(0, c * CHUNK, CHUNK)
-            scatter(1, c * CHUNK, CHUNK)
-        for t in (0, 1):
-            nc.sync.dma_start(out=out_rows[:, t, :], in_=y[t][:])
-            for q in range(4):
-                cast(t, q, nc.scalar.copy)
-        scatter(2, 0, J)
-        nc.sync.dma_start(out=out_rows[:, 2, :], in_=y[2][:])
-        for q in range(4):
-            if q < 2:
-                nc.scalar.copy(
-                    out=pairs[q][:, 1, :, :],
-                    in_=y[2][:, q * QUARTER : (q + 1) * QUARTER].unsqueeze(2).to_broadcast([P, QUARTER, 2]),
-                )
-            else:
-                cast(2, q, nc.scalar.copy)
-        scatter(3, 0, J)
-        nc.sync.dma_start(out=out_rows[:, 3, :], in_=y[3][:])
+        def round_rows(t, q, engine_copy):
+            engine_copy(out=pairs[q][:, t // 2, :, t % 2], in_=y[t][:, quarter_cols(q)])
 
         def weave(q, engine_copy):
             engine_copy(
@@ -225,23 +211,43 @@ def tile_moe_expert_hidden_taps_scattered_pl_kernel(
                 in_=pairs[q][:].rearrange("p u c e -> p u (c e)").bitcast(F32).rearrange("p u c -> p c u"),
             )
 
-        for q in (0, 1):
-            cast(3, q, nc.vector.tensor_copy)
-        for q in (0, 1):
-            weave(q, nc.vector.tensor_copy)
-        for q in (2, 3):
-            cast(3, q, nc.scalar.copy)
-        for q in (2, 3):
-            weave(q, nc.scalar.copy)
+        vector_quarters, scalar_quarters = (0, 1), (2, 3)
+
+        for c in range(CHUNKS):
+            scatter(0, c * CHUNK, CHUNK)
+            scatter(1, c * CHUNK, CHUNK)
+        for t in (0, 1):
+            nc.sync.dma_start(out=out_rows[:, t, :], in_=y[t][:])
+            for q in range(4):
+                round_rows(t, q, nc.scalar.copy)
+        scatter(2, 0, J)
+        nc.sync.dma_start(out=out_rows[:, 2, :], in_=y[2][:])
+        for q in vector_quarters:
+            nc.scalar.copy(
+                out=pairs[q][:, 1, :, :],
+                in_=y[2][:, quarter_cols(q)].unsqueeze(2).to_broadcast([P, QUARTER, 2]),
+            )
+        for q in scalar_quarters:
+            round_rows(2, q, nc.scalar.copy)
+        scatter(3, 0, J)
+        nc.sync.dma_start(out=out_rows[:, 3, :], in_=y[3][:])
+
+        for quarters, engine_copy in ((vector_quarters, nc.vector.tensor_copy), (scalar_quarters, nc.scalar.copy)):
+            for q in quarters:
+                round_rows(3, q, engine_copy)
+            for q in quarters:
+                weave(q, engine_copy)
+
         words_out = out_1[0].rearrange("p c t -> p (c t)").bitcast(I32)
+        stored = 0
         for q in range(4):
-            cols = slice(q * QUARTER, (q + 1) * QUARTER)
+            cols = quarter_cols(q)
             nc.vector.quantize_mx(
                 out=y_w[:, cols].bitcast(FP8X4), scales=y_s[:, cols], in_=y_bf[q][:].rearrange("p c t -> p (c t)")
             )
-            if q > 0:
-                done = slice(0 if q == 1 else q * QUARTER, (q + 1) * QUARTER)
-                nc.sync.dma_start(out=words_out[:, done], in_=y_w[:, done].bitcast(I32))
+            if q >= vector_quarters[-1]:
+                nc.sync.dma_start(out=words_out[:, stored : cols.stop], in_=y_w[:, stored : cols.stop].bitcast(I32))
+                stored = cols.stop
         rows_out = out_2[0].bitcast(I32).rearrange("(q r) c -> r q c", r=4)
         for r in range(4):
             queue = nc.scalar if r % 2 else nc.sync

from contextlib import ExitStack

import concourse.mybir as mybir

K, T, J, R, N = 512, 1024, 512, 512, 512
FLOPS = 2 * K * R * J + 2 * R * N * J

F32 = mybir.dt.float32
BF16 = mybir.dt.bfloat16
I32 = mybir.dt.int32
U32 = mybir.dt.uint32
U16 = mybir.dt.uint16
U8 = mybir.dt.uint8
FP8X4 = mybir.dt.float8_e4m3fn_x4
FP4X4 = mybir.dt.float4_e2m1fn_x4
MULT = mybir.AluOpType.mult
ADD = mybir.AluOpType.add
RELU = mybir.ActivationFunctionType.Relu
COPY = mybir.ActivationFunctionType.Copy

P = 128
PACK = 4
CHUNK = 128
CHUNKS = J // CHUNK
GATHERS = (128, 128, 256)
LIST_ROWS = 16
AHEAD = 2
QUARTER = T // 4
LINE = 4

WB_AT, ZEROS_AT, DC_AT, GA_AT = 0, 768, 1024, 1088


def load_scale_rows(nc, plane, scales):
    rows = scales[0].bitcast(I32).rearrange("(q r) c -> r q c", r=4)
    for r in range(4):
        nc.sync.dma_start(out=plane[r:P:32, :].bitcast(I32), in_=rows[r])


def deal_columns(nc, dealt, plain):
    nc.vector.tensor_copy(
        out=dealt.rearrange("p (t m) -> p t m", t=PACK),
        in_=plain.rearrange("p (m t) -> p t m", t=PACK),
    )


def tile_moe_expert_hidden_taps_scattered_pl_kernel(
    tc, xt_words, xt_scales, wa_words, wa_scales, dc, wb_words, wb_scales, ga, offs, out_0, out_1, out_2
):
    nc = tc.nc
    with ExitStack() as ctx:
        sb = ctx.enter_context(tc.tile_pool(name="sb", bufs=1))
        late = ctx.enter_context(tc.tile_pool(name="late", bufs=1))
        ps = ctx.enter_context(tc.psum_pool(name="ps", bufs=1))

        offsets = sb.tile([P, J // LIST_ROWS], U16, name="offsets")
        x_w = sb.tile([P, T], U16, name="x_w", align_bytes=64)
        x_s = sb.tile([P, T], U8, name="x_s", align_bytes=64)
        wa_w = sb.tile([P, R], I32, name="wa_w", align_bytes=64)
        w_s = sb.tile([P, R + N], U8, name="w_s", align_bytes=64)
        wa_s, wb_s = w_s[:, :R], w_s[:, R:]
        zeros = late.tile([P, P], F32, name="zeros", align_bytes=64, offset=ZEROS_AT)
        wb_w = late.tile([P, N], U16, name="wb_w", align_bytes=64, offset=WB_AT)
        dc_sb = late.tile([P, PACK], F32, name="dc_sb", align_bytes=64, offset=DC_AT)
        ga_col = late.tile([P, PACK], F32, name="ga_col", align_bytes=64, offset=GA_AT)
        ga_sb = sb.tile([P, J], F32, name="ga_sb", align_bytes=64)
        wb_wd = sb.tile([P, N], U16, name="wb_wd", align_bytes=64)
        wb_sd = sb.tile([P, N], U8, name="wb_sd", align_bytes=64)
        ident = sb.tile([P, P], F32, name="ident", align_bytes=64)
        tap = sb.tile([P, PACK, J], F32, name="tap", align_bytes=64)
        p_sb = sb.tile([P, PACK, J], F32, name="p_sb", align_bytes=64)
        pairs = [sb.tile([P, 2, QUARTER, 2], BF16, name="pairs%d" % q, align_bytes=64) for q in range(4)]
        y_bf = [sb.tile([P, QUARTER, PACK], BF16, name="y_bf%d" % q, align_bytes=64) for q in range(4)]
        y_w = sb.tile([P, T], U32, name="y_w", align_bytes=64)
        y_s = sb.tile([P, T], U8, name="y_s", align_bytes=64)

        nc.vector.memset(x_s[:].bitcast(I32), 0)
        nc.vector.memset(w_s[:].bitcast(I32), 0)
        nc.gpsimd.memset(zeros[:], 0.0)
        nc.gpsimd.affine_select(
            out=ident[:],
            in_=zeros[:],
            compare_op=mybir.AluOpType.not_equal,
            fill=1.0,
            base=0,
            pattern=[[-1, P]],
            channel_multiplier=1,
        )
        nc.vector.memset(tap[:, :, 0:1], 0.0)

        nc.sync.dma_start(offsets[:], offs)
        nc.sync.dma_start(out=x_w[:].bitcast(I32), in_=xt_words[0].bitcast(I32))
        nc.sync.dma_start(out=wa_w[:], in_=wa_words[0].rearrange("p n t -> p (n t)").bitcast(I32))
        load_scale_rows(nc, x_s, xt_scales)
        load_scale_rows(nc, wa_s, wa_scales)
        nc.sync.dma_start(out=dc_sb[:], in_=dc.rearrange("(p t) o -> p (t o)", t=PACK))
        nc.sync.dma_start(out=ga_col[:], in_=ga.rearrange("o (p u) -> p (o u)", u=PACK))
        nc.sync.dma_start(out=wb_w[:].bitcast(I32), in_=wb_words[0].bitcast(I32))
        load_scale_rows(nc, wb_s, wb_scales)

        def listed(j0, count):
            return offsets[:, j0 // LIST_ROWS : (j0 + count) // LIST_ROWS]

        tokens = []
        for g, count in enumerate(GATHERS):
            entries = listed(sum(GATHERS[:g]), count)
            g_w = sb.tile([P, count], U16, name="g_w%d" % g, align_bytes=64)
            g_s = sb.tile([P, count], U8, name="g_s%d" % g, align_bytes=64)
            nc.vector.tensor_copy(g_w[:], x_w[:].indirect(entries))
            nc.vector.tensor_copy(g_s[:], x_s[:].indirect(entries))
            for c0 in range(0, count, CHUNK):
                tokens.append((g_w[:, c0 : c0 + CHUNK], g_s[:, c0 : c0 + CHUNK]))

        h_w = sb.tile([P, J], U32, name="h_w", align_bytes=64)
        h_s = sb.tile([P, J], U8, name="h_s", align_bytes=64)

        def first_layer(c):
            j0, j1 = c * CHUNK, (c + 1) * CHUNK
            chunk_w, chunk_s = tokens[c]
            a_t = ps.tile([P, R], F32, name="a_t", bufs=2)
            nc.tensor.matmul_mx(
                out=a_t[:],
                lhsT=chunk_w.bitcast(FP4X4),
                lhsT_scale=chunk_s,
                rhs=wa_w[:].bitcast(FP8X4),
                rhs_scale=wa_s,
                start=True,
                stop=True,
            )
            h_t = sb.tile([P, PACK, P], F32, name="h_t", bufs=2, align_bytes=64)
            nc.scalar.activation(out=h_t[:], in_=a_t[:].rearrange("j (m t) -> j t m", t=PACK), func=RELU)
            h1 = ps.tile([P, PACK, CHUNK], F32, name="h1", bufs=3)
            for t in range(PACK):
                nc.tensor.transpose(h1[:, t, :], h_t[:, t, :], ident[:])
            kept = min(j1, J - 1) - j0
            for t in range(PACK):
                shifted = tap[:, t, j0 + 1 : j0 + 1 + kept]
                if c == 0:
                    nc.vector.tensor_scalar(
                        out=shifted, in0=h1[:, t, :kept], scalar1=dc_sb[:, t : t + 1], scalar2=None, op0=MULT
                    )
                else:
                    nc.scalar.activation(out=shifted, in_=h1[:, t, :kept], func=COPY, scale=dc_sb[:, t : t + 1])
            hid = sb.tile([P, CHUNK, PACK], BF16, name="hid%d" % c, align_bytes=64)
            nc.vector.tensor_tensor(
                out=hid[:].rearrange("p (g i) t -> p g t i", i=LINE),
                in0=h1[:].rearrange("p t (g i) -> p g t i", i=LINE),
                in1=tap[:, :, j0:j1].rearrange("p t (g i) -> p g t i", i=LINE),
                op=ADD,
            )
            nc.vector.quantize_mx(
                out=h_w[:, j0:j1].bitcast(FP8X4), scales=h_s[:, j0:j1], in_=hid[:].rearrange("p j t -> p (j t)")
            )

        def second_layer(row_sets, j0, j1):
            acc = ps.tile([P, len(row_sets), j1 - j0], F32, name="acc", bufs=3)
            for u, t in enumerate(row_sets):
                cols = slice(t * P, (t + 1) * P)
                nc.tensor.matmul_mx(
                    out=acc[:, u, :],
                    lhsT=wb_wd[:, cols].bitcast(FP4X4),
                    lhsT_scale=wb_sd[:, cols],
                    rhs=h_w[:, j0:j1].bitcast(FP8X4),
                    rhs_scale=h_s[:, j0:j1],
                    start=True,
                    stop=True,
                )
            nc.scalar.copy(out=p_sb[:, row_sets[0] : row_sets[-1] + 1, j0:j1], in_=acc[:])

        first_layer(0)
        deal_columns(nc, wb_wd[:], wb_w[:])
        deal_columns(nc, wb_sd[:], wb_s)

        spread = ps.tile([P, PACK, P], F32, name="acc", bufs=3)
        for u in range(PACK):
            nc.tensor.transpose(spread[:, u, :], ga_col[:, u : u + 1].to_broadcast([P, P]), ident[:])
        nc.scalar.copy(out=ga_sb[:].rearrange("p (n u) -> p n u", u=PACK), in_=spread[:].rearrange("p u n -> p n u"))

        for c in range(1, CHUNKS + AHEAD):
            if c < CHUNKS:
                first_layer(c)
            if c >= AHEAD:
                second_layer((0, 1), (c - AHEAD) * CHUNK, (c - AHEAD + 1) * CHUNK)
        second_layer((2,), 0, J)
        second_layer((3,), 0, J)

        y = []
        for t in range(PACK):
            y.append(sb.tile([P, T], F32, name="y%d" % t, align_bytes=64))
            nc.gpsimd.memset(y[t][:].bitcast(I32), 0)

        out_rows = out_0.rearrange("(p t) c -> p t c", t=PACK)

        def scatter(t, j0, count):
            nc.vector.tensor_tensor(
                y[t][:].indirect(listed(j0, count)),
                p_sb[:, t, j0 : j0 + count],
                ga_sb[:, j0 : j0 + count],
                MULT,
            )

        def quarter_cols(q):
            return slice(q * QUARTER, (q + 1) * QUARTER)

        def round_rows(t, q, engine_copy):
            engine_copy(out=pairs[q][:, t // 2, :, t % 2], in_=y[t][:, quarter_cols(q)])

        def weave(q, engine_copy):
            engine_copy(
                out=y_bf[q][:].rearrange("p c t -> p (c t)").bitcast(F32).rearrange("p (c u) -> p c u", u=2),
                in_=pairs[q][:].rearrange("p u c e -> p u (c e)").bitcast(F32).rearrange("p u c -> p c u"),
            )

        vector_quarters, scalar_quarters = (0, 1), (2, 3)

        for c in range(CHUNKS):
            scatter(0, c * CHUNK, CHUNK)
            scatter(1, c * CHUNK, CHUNK)
        for t in (0, 1):
            nc.sync.dma_start(out=out_rows[:, t, :], in_=y[t][:])
            for q in range(4):
                round_rows(t, q, nc.scalar.copy)
        scatter(2, 0, J)
        nc.sync.dma_start(out=out_rows[:, 2, :], in_=y[2][:])
        for q in vector_quarters:
            nc.scalar.copy(
                out=pairs[q][:, 1, :, :],
                in_=y[2][:, quarter_cols(q)].unsqueeze(2).to_broadcast([P, QUARTER, 2]),
            )
        for q in scalar_quarters:
            round_rows(2, q, nc.scalar.copy)
        scatter(3, 0, J)
        nc.sync.dma_start(out=out_rows[:, 3, :], in_=y[3][:])

        for quarters, engine_copy in ((vector_quarters, nc.vector.tensor_copy), (scalar_quarters, nc.scalar.copy)):
            for q in quarters:
                round_rows(3, q, engine_copy)
            for q in quarters:
                weave(q, engine_copy)

        words_out = out_1[0].rearrange("p c t -> p (c t)").bitcast(I32)
        stored = 0
        for q in range(4):
            cols = quarter_cols(q)
            nc.vector.quantize_mx(
                out=y_w[:, cols].bitcast(FP8X4), scales=y_s[:, cols], in_=y_bf[q][:].rearrange("p c t -> p (c t)")
            )
            if q >= vector_quarters[-1]:
                nc.sync.dma_start(out=words_out[:, stored : cols.stop], in_=y_w[:, stored : cols.stop].bitcast(I32))
                stored = cols.stop
        rows_out = out_2[0].bitcast(I32).rearrange("(q r) c -> r q c", r=4)
        for r in range(4):
            queue = nc.scalar if r % 2 else nc.sync
            queue.dma_start(out=rows_out[r], in_=y_s[r:P:32, :].bitcast(I32))
